import numpy as np, ml_dtypes
CORES = [66,74,82,90,194,202,210,218]
N = 8
BF = ml_dtypes.bfloat16
def gentries(a):
    return np.ascontiguousarray(a.reshape(8, 16, -1).transpose(0, 2, 1)).reshape(8, -1)
def gtable(e):
    e = np.asarray(e); return np.ascontiguousarray(e.reshape(8, -1, 16).transpose(0, 2, 1)).reshape(128, -1).astype(np.int32)
W, R, NR, TV = 2048, 32, 128, 3
K = R * NR; NONE = W - 1; SH = (N, 8, R, NR)
def hsh(a, b):
    return (((a * b) >> 5) + 37 * a + b) & (W - 1)
def pack(x, y, g, a, b, t):
    o = {"xt": np.ascontiguousarray(x.reshape(N, 128, W)).astype(np.float32).astype(BF), "yv": np.ascontiguousarray(y.reshape(N, 128, TV * NR)).astype(np.float32).astype(BF)}
    for k, v in (("gl", g), ("al", a), ("bl", b), ("th", t)): o[k] = np.stack([gtable(w.reshape(8, -1)) for w in v])
    return o
def robots(rng, share, mem):
    g = np.where(rng.random(SH) < share, rng.integers(0, NONE, SH), NONE); keep = rng.random(SH) < mem
    return g, np.where(keep, rng.integers(0, NONE, SH), NONE), np.where(keep, rng.integers(0, NONE, SH), NONE)
def pool(rng, goals, m):
    a = rng.permutation(NONE)[:64]; a[0] = 64; a[1] = 128
    lut = np.zeros(W, bool); lut[goals] = True
    i, j = np.nonzero(lut[hsh(a[:, None], np.arange(NONE)[None, :])]); s = rng.integers(0, len(i), m)
    return a[i[s]], j[s]
def halves(rng, x, y, q, e):
    near = np.zeros(W, bool); near[rng.permutation(NONE)[:W // 2]] = True
    x[q, e] = np.where(near[None, :], rng.integers(0, 64, (16, W)), rng.integers(128, 256, (16, W)))
    y[q, e, :, 0] = rng.integers(0, 64, (16, NR))
    return near
def pairs(rng, near):
    far = rng.permutation(np.nonzero(~near[:NONE])[0]); a = far[:128]
    i, j = np.nonzero(near[hsh(a[:, None], far[None, :])]); s = rng.permutation(len(i))
    u, v = a[i[s]], far[j[s]]
    return u, v, hsh(u, v)
def setup_inputs(rng):
    x = rng.integers(0, 256, (N, 8, 16, W)); y = rng.integers(0, 256, (N, 8, 16, TV, NR))
    g, a, b = robots(rng, rng.choice(np.array([0.3, 0.6, 0.9, 1.0]), (N, 8, 1, NR)), 0.4)
    return pack(x, y, g, a, b, rng.integers(900, 1700, SH))
def setup_inputs_clash(rng):
    x = rng.integers(0, 256, (N, 8, 16, W)); y = rng.integers(0, 256, (N, 8, 16, TV, NR)); g, a, b = robots(rng, 1.0, 0.3)
    for q in range(N):
        for e in range(8):
            goals = np.concatenate([np.array([0, W - 2]), rng.integers(1, W - 2, 2)]); c = rng.integers(0, 256, 16)
            x[q, e][:, goals] = c[:, None]; y[q, e][:, 0, :] = c[:, None]
            u, v = pool(rng, goals, (R // 2) * NR)
            g[q, e, 0::2] = u.reshape(R // 2, NR); g[q, e, 1::2] = v.reshape(R // 2, NR)
    g = np.where((rng.random((N, 8, 1, NR)) < 0.3) | (rng.random(SH) < 0.1), NONE, g)
    for q in range(N):
        for s, e in enumerate(rng.permutation(8)[:2]):
            u, v, n = pairs(rng, halves(rng, x, y, q, e))
            if s == 0:
                w = np.nonzero(n == n[0])[0]; i = w[rng.integers(0, len(w), K // 2)]
            else:
                i = rng.integers(0, len(n), K // 2); i[:NR] = rng.permutation(np.unique(n, return_index=True)[1])[:NR]
            g[q, e, 0::2] = u[i].reshape(R // 2, NR); g[q, e, 1::2] = v[i].reshape(R // 2, NR)
    return pack(x, y, g, a, b, rng.integers(900, 1700, SH))
def setup_inputs_ties(rng):
    s = rng.integers(0, 2, (N, 8, 1, 1)) * 3 + 1
    x = 100 + s * rng.integers(0, 8, (N, 8, 16, W)); y = 100 + s[..., None] * rng.integers(0, 8, (N, 8, 16, TV, NR))
    g, a, b = robots(rng, rng.choice(np.array([0.4, 0.7, 1.0]), (N, 8, 1, NR)), 0.6)
    return pack(x, y, g, a, b, np.where(s == 1, rng.integers(0, 60, SH), rng.integers(60, 200, SH)))
def setup_inputs_corners(rng):
    x = rng.integers(0, 256, (N, 8, 16, W)); y = rng.integers(0, 256, (N, 8, 16, TV, NR)); g, a, b = robots(rng, 1.0, 1.0)
    kd = rng.integers(0, 11, (N, 8, 1, NR)); k = np.arange(R)[None, None, :, None]
    none = g.copy()
    for q in range(N):
        for e in range(8):
            u, v = pool(rng, np.array([NONE]), (R // 2) * NR)
            none[q, e, 0::2] = u.reshape(R // 2, NR); none[q, e, 1::2] = v.reshape(R // 2, NR)
    g = np.where(kd == 6, g[:, :, :1], np.where(kd == 8, none, np.where((kd == 10) & (k % 2 == 0), 0, g)))
    full = (kd == 1) | ((kd == 2) & (k % 2 == 0)) | ((kd == 3) & (k % 2 == 1)) | ((kd == 4) & (k == R - 1)) | ((kd == 5) & (k == 0)) | (kd == 6) | ((kd == 7) & (k % 4 < 2)) | (kd == 8) | ((kd == 9) & (rng.random(SH) < 0.5)) | (kd == 10)
    g = np.where(full, g, NONE)
    a = np.where((kd == 9) | ((kd == 10) & (rng.random(SH) < 0.5)), NONE, a); b = np.where(kd == 7, NONE, b)
    a = np.where(rng.random(SH) < 0.05, rng.choice(np.array([0, W - 2]), SH), a)
    t = rng.choice(np.array([0, 4080, 1300, 1400]), SH, p=[0.3, 0.2, 0.25, 0.25])
    for q in range(N):
        for s, e in enumerate(rng.permutation(8)[:2]):
            near = halves(rng, x, y, q, e); far = np.nonzero(~near[:NONE])[0]
            second = (np.arange(R)[:, None] + rng.integers(0, 2, NR)[None, :]) % 2 == 0
            if s == 0:
                a[q, e] = rng.integers(0, NONE, (R, NR)); t[q, e] = rng.integers(0, 1000, (R, NR))
            else:
                far = far[near[hsh(NONE, far)]]; w = rng.random((R, NR)) < 0.5
                a[q, e] = np.where(w, NONE, a[q, e]); t[q, e] = np.where(w, t[q, e], 4080)
            g[q, e] = np.where(second, far[rng.integers(0, len(far), (R, NR))], NONE)
    return pack(x, y, g, a, b, t)
def setup_inputs_ends(rng):
    v = 255 * rng.integers(0, 2, (N, 1, 1, 1)); e = rng.integers(0, 4, (N, 8, 1, W))
    x = np.where(e == 0, 0, np.where(e == 1, 255, 255 * rng.integers(0, 2, (N, 8, 16, W))))
    near = (rng.random((N, 8, 1, W)) < 0.25) & (np.arange(16)[None, None, :, None] == rng.integers(0, 16, (N, 8, 1, W)))
    x = np.where(near, np.abs(x - 1), x)
    x[..., 0] = v[..., 0]; x[..., W - 2] = v[..., 0]; x[..., W - 74] = 255 - v[..., 0]
    e = rng.integers(0, 3, (N, 8, 1, TV, NR)); y = np.where(e == 0, 0, np.where(e == 1, 255, 255 * rng.integers(0, 2, (N, 8, 16, TV, NR))))
    S = np.array([0, 1, int(rng.integers(2, NR - 2)), NR - 2, NR - 1])
    k = np.arange(R)[None, None, :, None]
    ty = rng.choice(np.array([0, 1, 2]), (N, 8, 1, NR), p=[0.6, 0.3, 0.1])
    ty[..., S] = 1
    g = np.where(ty == 0, rng.choice(np.array([0, NONE]), SH), np.where(ty == 1, np.where(k % 2 == 0, W - 2, 0), np.where(rng.random(SH) < 0.3, NONE, rng.integers(0, NONE, SH))))
    a = rng.choice(np.array([0, NONE, W - 2]), SH, p=[0.45, 0.45, 0.1]); b = rng.choice(np.array([0, NONE, W - 2]), SH, p=[0.45, 0.45, 0.1])
    t = rng.choice(np.array([0, 4080, 4079, 1]), SH, p=[0.4, 0.4, 0.1, 0.1])
    far = np.roll(v, -1, axis=0)
    for i in S:
        y[:, :, :, 0, i] = 255 - v[..., 0]; y[:, :, :, 1, i] = 255 - far[..., 0]
        t[:, :, :, i] = 4080 - 4 * R - (np.arange(R)[None, None, :] // 2) % 2
    return pack(x, y, g, a, b, t)
def setup_inputs_spread(rng):
    x = np.minimum((np.exp2(8 * rng.random((N, 8, 1, W))) * rng.random((N, 8, 16, W))).astype(np.int64), 255)
    y = np.minimum((np.exp2(8 * rng.random((N, 8, 1, TV, NR))) * rng.random((N, 8, 16, TV, NR))).astype(np.int64), 255)
    g, a, b = robots(rng, rng.random((N, 8, 1, NR)), rng.random((N, 8, 1, NR)))
    few = rng.random((N, 8, 1, NR)) < 0.5
    g = np.where(few & (g != NONE), np.minimum((NONE * rng.random(SH) ** 6).astype(np.int64), NONE - 1), g)
    t = np.minimum(np.exp2(12 * rng.random(SH)).astype(np.int64) - 1, 4080)
    return pack(x, y, g, a, b, t)
def check_inputs(d):
    bad = []
    for k, hi in (("xt", 255), ("yv", 255), ("gl", NONE), ("al", NONE), ("bl", NONE), ("th", 4080)):
        v = np.asarray(d[k]).astype(np.float64)
        if not (np.all(v >= 0) and np.all(v <= hi)): bad.append("range of " + k)
        elif np.any(v != np.floor(v)): bad.append("whole numbers of " + k)
    return bad
def reference(xt, yv, gl, al, bl, th):
    x = xt.astype(np.float32).astype(np.int32).reshape(N, 8, 16, W); y = yv.astype(np.float32).astype(np.int32).reshape(N, 8, 16, TV, NR)
    g, a, b, h = [np.stack([gentries(v) for v in w]).astype(np.int32).reshape(N, 8, R, NR) for w in (gl, al, bl, th)]
    c = np.zeros((N, NR), np.int32); row = np.arange(R)[None, :, None]; rob = np.arange(NR)[None, :]
    for t in range(TV):
        for r in range(N):
            q = (r + t) % N; G, A, B = g[r].copy(), a[r].copy(), b[r].copy()
            G1 = np.roll(G, -1, axis=1); n = hsh(G, G1); view = y[r][:, :, t][:, :, None, :]
            xg = np.take_along_axis(x[q], G.reshape(8, 1, K), 2); xn = np.take_along_axis(x[q], n.reshape(8, 1, K), 2)
            dg = np.add.reduce(np.abs(xg.reshape(8, 16, R, NR) - view), axis=1); dn = np.add.reduce(np.abs(xn.reshape(8, 16, R, NR) - view), axis=1)
            dg1 = np.roll(dg, -1, axis=1); full = G != NONE; full1 = np.roll(full, -1, axis=1)
            opens = full & (A != NONE) & ~full1 & (dg > h[r] + c[r][None, None, :])
            opened = np.roll(opens, 1, axis=1)
            merge = full & full1 & ~np.roll(opens, -1, axis=1) & ((row + t) % 2 == 0) & (n != NONE) & (dn < np.minimum(dg, dg1))
            gone = np.roll(merge, 1, axis=1)
            take = ~full & ~opened & full1 & (n != NONE) & (dn < dg1)
            some = np.any(merge, axis=1); low = np.argmax(merge, axis=1)
            i0 = low * NR + rob; i1 = ((low + 1) % R) * NR + rob
            val = (np.take_along_axis(xg, i0[:, None, :], 2) + np.take_along_axis(xg, i1[:, None, :], 2)) >> 1
            goal = np.take_along_axis(n.reshape(8, K), i0, 1)
            for e in range(8):
                w = np.nonzero(some[e])[0]; u, first = np.unique(goal[e][w], return_index=True)
                x[q, e][:, u] = val[e][:, w[first]]
            clear = opens | opened | gone | take
            g[r] = np.where(opens, A, np.where(opened, np.roll(B, 1, axis=1), np.where(merge | take, n, np.where(gone, NONE, G))))
            na = np.where(merge, G, np.where(clear, NONE, A)); nb = np.where(merge, G1, np.where(clear, NONE, B))
            a[r] = na; b[r] = nb; c[r] = np.add.reduce(merge.astype(np.int32), axis=(0, 1))
    o = [np.stack([gtable(v.reshape(8, -1)) for v in w]).astype(np.float32) for w in (g, a, b)]
    return {"og": o[0], "oa": o[1], "ob": o[2], "ox": x.reshape(N, 128, W).astype(np.float32).astype(BF)}

from concourse.mybir import AluOpType as A
from concourse.mybir import ActivationFunctionType as F

U = 128
NONE = 2047
WT = 2048 + 128
BIG = 32768.0
FAR = 1024.0
CH = [(0, 0, 64), (0, 64, 128), (1, 0, 64), (1, 64, 128), (2, 0, 64), (2, 64, 96), (2, 96, 128)]

SCRATCH = {}


def _add(where, dtype, **kw):
    for k, v in kw.items():
        SCRATCH[k] = (where, [128] + (v if isinstance(v, list) else [v]), dtype)


_add("sbuf", "bfloat16", tab0=WT, tab1=WT, tab2=WT, xsav=16, yvs=384, vx0=1024, vx1=1024, vx2=1024,
     bo=128, lall=2048, ib=128, eq=1024, sc=1024, rst=1024, cs=128,
     val0=128, val1=128, val2=128, a1v=128, a2v=128, b2v=128, b0v=128, c0v=128)
for _k in range(len(CH)):
    _add("sbuf", "bfloat16", **{"df%d" % _k: (CH[_k][2] - CH[_k][1]) * 16})
_add("sbuf", "int32", gli=[32, 8], ali=[32, 8], bli=[32, 8], thi=[32, 8], pidx=8, p15=8, p4=8,
     hb=128, pp=128, ny=128, sh=128, tt_=128, nxi=128, ki=24, gi=24, vi=128)
_add("sbuf", "uint16", off=384, goff=24, lw0=8, lw1=8, lw2=8, a1l=8, a2l=8, b2l=8, b0l=8, c0l=8)
_add("sbuf", "float16", gx0=136, gx1=136, gy0=128, gy1=128, abx0=256, abx1=256, aby0=256, aby1=256, ab2=256,
     ex=136, ey=128, ax=128, ay=128, qy=128, nx=128, rr=128, ids=896,
     ones=128, jc=128, oxf=128, oyp=136, mm=256, tx=128, ty=128, prod=1024)
_add("sbuf", "float32", tha=128, thb=128, id32=128, ca=128, cb=128, cj=128, prow=8, pgrp=8, cc=8, dum=8, fb=[3, 8],
     maskd=128, iw=WT, sgx=136, sqy=128, mn=128, mnm=128, mt=128, kn=384, k0=[3, 128], k1=[3, 64], k2=[3, 32],
     k3=[3, 16], k4=[3, 8], k5=[3, 8], gf=8, bf=128, bd=128, xv=256, lm=8, lf=8,
     ogs=[32, 8], oas=[32, 8], obs=[32, 8])
_add("psum", "float32", **{"b%d" % k: 512 for k in range(8)})
SEMAPHORES = ["pv", "pa", "pt", "pg", "dg", "dy", "dx", "da", "db", "dt", "og_", "oa_", "ob_", "ox_", "tl", "ls",
              "t1", "t2"] + [s + k + "_" for s in ("a1", "a2", "b2", "b0", "c0") for k in "vl"]
PART = {k: ("prod", U * j) for j, k in enumerate(("p1", "p2", "p3", "p4_", "p5", "p6", "p7", "p8"))}
PART.update({k: ("ids", U * j) for j, k in enumerate(("id1", "idm", "id37", "id2047", "idn2047", "idbig", "idnbig"))})
BANKS = ["b%d" % k for k in range(8)]


def rank_program(g, core, T, topo):
    rank = T.rank_of(core)
    if rank is None:
        return
    n = len(T.cores)
    Q = {"V": g.vector, "S": g.scalar, "P": g.tensor, "G": g, "Y": g.sync}
    PS = {"V": "pv", "S": "pa", "P": "pt", "G": "pg"}
    cnt = {"V": 0, "S": 0, "P": 0, "G": 0}
    known = {e: {} for e in Q}
    wr, rd, bank = {}, {}, {}

    def wait(e, toks):
        for eng, sem, val, snap in toks:
            if known[e].get(sem, 0) >= val:
                continue
            Q[e].wait_ge(T.sem[sem], val)
            for s, v in snap.items():
                if known[e].get(s, 0) < v:
                    known[e][s] = v
            known[e][sem] = val

    def hit(recs, lo, hi):
        return [r[2] for r in recs if r[0] < hi and lo < r[1]]

    def before(e, reads, writes):
        toks = []
        for b, lo, hi in reads:
            toks += hit(wr.get(b, []), lo, hi)
        for b, lo, hi in writes:
            w = hit(wr.get(b, []), lo, hi)
            toks += [t for t in w if not (e == "P" and t[0] == "P")]
            toks += hit(rd.get(b, []), lo, hi)
        for b, lo, hi in reads + writes:
            if b in bank:
                toks += [t for f, t in bank[b].items() if f != e]
        toks.sort(key=lambda t: -t[2])
        wait(e, toks)

    def after(e, reads, writes, tok):
        for b, lo, hi in writes:
            wr[b] = [r for r in wr.get(b, []) if not (lo <= r[0] and r[1] <= hi)] + [(lo, hi, tok)]
            rd[b] = [r for r in rd.get(b, []) if not (lo <= r[0] and r[1] <= hi)]
        for b, lo, hi in reads:
            rd[b] = [r for r in rd.get(b, []) if not (lo <= r[0] and r[1] <= hi and r[2][0] == e)] + [(lo, hi, tok)]
        for b, lo, hi in reads + writes:
            if b in BANKS:
                bank.setdefault(b, {})[e] = tok

    def landed(b, sem, val, e="D"):
        after(e, [], [(b, 0, 10 ** 6)], (e, sem, val, {}))

    def do(e, outs, ins, call):
        reads = [r for v in ins for r in v[1]]
        writes = [r for v in outs for r in v[1]]
        before(e, reads, writes)
        i = call(Q[e])
        cnt[e] += 1
        i.then_inc(T.sem[PS[e]], 1)
        snap = dict(known[e])
        after(e, reads, writes, (e, PS[e], cnt[e], snap))

    def B(b, lo=0, hi=U):
        if b in PART:
            b, o = PART[b]
            lo, hi = lo + o, hi + o
        return (T[b][:, lo:hi], [(b, lo, hi)])

    def X3(b, *ix):
        return (T[b][(slice(None),) + ix], [(b, 0, 10 ** 6)])

    ALL = slice(None)
    EV, OD = slice(0, 32, 2), slice(1, 32, 2)

    def ST(b, lo, hi, step):
        return (T[b][:, lo:hi:step], [(b, lo, hi)])

    def ind(w, o):
        return (w[0].indirect(o[0]), w[1] + o[1])

    def tt(o, a, b, op):
        do("V", [o], [a, b], lambda q: q.tensor_tensor(out=o[0], in0=a[0], in1=b[0], op=op))

    def ts(o, a, s1, op0, s2=None, op1=None):
        col = [s1] if isinstance(s1, tuple) else []
        x = s1[0] if col else s1
        if op1 is None:
            do("V", [o], [a] + col, lambda q: q.tensor_scalar(out=o[0], in0=a[0], scalar1=x, scalar2=None, op0=op0))
        else:
            do("V", [o], [a] + col, lambda q: q.tensor_scalar(out=o[0], in0=a[0], scalar1=x, scalar2=s2, op0=op0, op1=op1))

    def cp(o, a):
        do("V", [o], [a], lambda q: q.tensor_copy(out=o[0], in_=a[0]))

    def fill(o, x):
        do("V", [o], [], lambda q: q.memset(o[0], x))

    def act(o, a, func, scale=1.0, bias=0.0):
        do("S", [o], [a], lambda q: q.activation(out=o[0], in_=a[0], func=func, bias=bias, scale=scale))

    def mm(o, l, r, start, stop):
        do("P", [o], [l, r], lambda q: q.matmul(out=o[0], lhsT=l[0], rhs=r[0], start=start, stop=stop))

    def psum(bk, lo, terms):
        rots = [t[3] for t in terms]
        cuts = [(0, U)]
        if 1 in rots:
            cuts = [(0, 120), (120, U)]
        if -1 in rots:
            cuts = [(0, 8), (8, U)]
        for a, b in cuts:
            for k, (l, buf, c0, rot) in enumerate(terms):
                s = (a + 8 * rot) % U
                mm(B(bk, lo + a, lo + b), B(l), B(buf, c0 + s, c0 + s + b - a), k == 0, k == len(terms) - 1)

    def load(sem, b, src):
        g.sync.dma_start(out=T[b][(ALL,) * len(T[b].shape)] if b != "tab0" else T[b][:, 0:2048], in_=src).then_inc(T.sem[sem], 16)
        landed(b, sem, 16)

    load("dg", "gli", T.gl[:, :])
    load("dy", "yvs", T.yv[:, :])
    load("dx", "tab0", T.xt[:, :])
    load("da", "ali", T.al[:, :])
    load("db", "bli", T.bl[:, :])
    load("dt", "thi", T.th[:, :])

    def iota(o, pattern, base, cm, flag=True):
        if flag:
            do("G", [o], [], lambda q: q.iota(o[0], pattern, base, cm, allow_small_or_imprecise_dtypes=True))
        else:
            do("G", [o], [], lambda q: q.iota(o[0], pattern, base, cm))

    iota(B("pidx", 0, 8), [[16, 8]], 0, 1, False)
    iota(B("cb"), [[0, 8], [1, 16]], 0, 0)
    iota(B("ca"), [[1, 8], [0, 16]], 0, 0)
    iota(B("cj"), [[4096, 16], [0, 8]], 0, 0)
    iota(B("cc", 0, 8), [[16, 8]], 2048, 0)

    fill(B("lall", 0, 2048), 0.0)
    fill(B("eq", 0, 1024), 0.0)
    fill(B("rst", 0, 1024), 1.0)
    fill(ST("rst", 0, 1024, 128), 0.0)
    fill(X3("fb", slice(1, 3), ALL), 0.25)
    ts(B("p15", 0, 8), B("pidx", 0, 8), 15, A.bitwise_and)
    ts(B("p4", 0, 8), B("pidx", 0, 8), 4, A.arith_shift_right)
    cp(B("prow", 0, 8), B("p15", 0, 8))
    cp(B("pgrp", 0, 8), B("p4", 0, 8))
    ts(B("rr"), B("cb"), B("prow", 0, 1), A.is_equal)
    ts(B("bo"), B("ca"), B("pgrp", 0, 1), A.is_equal)
    tt(B("id1"), B("bo"), B("rr"), A.mult)
    for b, x in (("id37", 37.0), ("idm", -1.0), ("id2047", 2047.0), ("idn2047", -2047.0), ("idbig", BIG), ("idnbig", -BIG)):
        ts(B(b), B("id1"), x, A.mult)
    ts(B("ones"), B("rr"), 0.0, A.mult, 1.0, A.add)

    def late_consts():
        for a in range(8):
            cp((T.lall[:, 16 * a:16 * a + 129 * 15 + 1:129], [("lall", 0, 2048)]), B("bo", 16 * a, 16 * a + 16))
        cp(B("jc"), B("cj"))
        cp(B("id32"), B("id1"))
        cp(B("ib"), B("id1"))
        ts(B("maskd"), B("cb"), B("prow", 0, 1), A.is_ge, 4096.0, A.mult)
        tt(B("dum", 0, 8), B("prow", 0, 8), B("cc", 0, 8), A.add)
        ts(X3("fb", 0, ALL), B("dum", 0, 8), 65536.0, A.add, 2.0 ** -18, A.mult)

    def views(t):
        v = "vx%d" % t
        act(B(v, 0, 128), B("yvs", t * 128, t * 128 + 128), F.Copy)
        for w in (128, 256, 512):
            act(B(v, w, 2 * w), B(v, 0, w), F.Copy)

    def lists(t, ysrc):
        gx, gy = "gx%d" % (t % 2), "gy%d" % (t % 2)
        ts(B("ey"), B(gy), 2047.0, A.is_equal)
        cp(B("off", 0, 128), B(gx))
        psum("b1", 0, [("id37", gx, 0, 0), ("id1", gy, 0, 0)])
        psum("b1", 128, [("id2047", "ones", 0, 0), ("idn2047", "ey", 0, 0)])
        tt(B("pp"), B(gx), ysrc, A.mult)
        ts(B("hb"), B(gx, 8, 136), 64.96875, A.mult, 75738.515625, A.add)
        ts(B("sh"), B("pp"), 5, A.arith_shift_right)
        ts(B("ny"), B("hb"), 2047, A.bitwise_and)
        tt(B("tt_"), B("sh"), B("b1"), A.add)
        tt(B("b7"), B("ny"), B("b1", 128, 256), A.max)
        ts(B("nxi"), B("tt_"), 2047, A.bitwise_and)
        tt(B("qy"), B("b7"), B(gy), A.min)
        cp(B("nx"), B("nxi"))
        cp(B("off", 128, 256), B("qy"))
        cp(B("off", 256, 384), B("nx"))
        ts(B("ex", 0, 136), B(gx, 0, 136), 2047.0, A.is_equal)

    def prepare(t):
        s = t % 2
        gx, gy, abx, aby = "gx%d" % s, "gy%d" % s, "abx%d" % s, "aby%d" % s
        ts(B("ax"), B(abx), 2047.0, A.is_equal)
        ts(B("ay"), B(aby), 2047.0, A.is_equal)
        for k, (src, gb) in enumerate((("nx", 0), (gx, 0), (gy, 0))):
            psum("b2", 128 * k, [("id1", src, 0, 0), ("id1", "jc", 0, 0)])
        act(B("kn", 0, 384), B("b2", 0, 384), F.Copy, scale=2.0 ** -18)
        c = [("ib", "cs", 0, 0)] if t else []
        hx, hy, rot = ("thb", "tha", 1) if t == 1 else ("tha", "thb", 0)
        psum("b3", 0, [("id32", hx, 0, 0), ("idbig", "ax", 0, 0), ("idbig", "ex", 0, 0), ("idnbig", "ey", 0, 0), ("idbig", "ones", 0, 0)] + c)
        psum("b3", 128, [("id32", hy, 0, rot), ("idbig", "ay", 0, 0), ("idbig", "ey", 0, 0), ("idnbig", "ex", 8, 0), ("idbig", "ones", 0, 0)] + c)
        psum("b5", 0, [("id1", abx, 0, 0), ("idm", gx, 0, 0)])
        psum("b5", 128, [("id1", aby, 128, -1), ("idn2047", "ones", 0, 0)])
        psum("b5", 256, [("id1", "nx", 0, 0), ("idm", gx, 0, 0)])
        psum("b5", 384, [("id1", abx, 128, 0), ("idn2047", "ones", 0, 0)])
        psum("b6", 0, [("id1", aby, 0, 0), ("idm", gy, 0, 0)])
        psum("b6", 128, [("id1", "qy", 0, 0), ("idn2047", "ones", 0, 0)])
        psum("b6", 256, [("id2047", "ones", 0, 0), ("idm", gy, 0, 0)])

    def contract(k):
        l, lo, hi = CH[k]
        d, w = "df%d" % k, (hi - lo) * 16
        for r in range(16):
            mm(B("b%d" % l, lo, hi), B("lall", 128 * r, 128 * r + 128),
               (T[d][:, r:w:16], [(d, 0, w)]), r == 0, r == 15)

    def scatter(tab, lst, val):
        w = B(tab, 0, WT)
        do("V", [w], [B(lst, 0, 8), B(val)],
           lambda q: q.tensor_copy(out=w[0].indirect(T[lst][:, 0:8]), in_=T[val][:, :]))

    ncall = [0]

    def send(dst, dbuf, dsem, sbuf, width, lsem="ls"):
        rid, pid = topo.addr(dst, core)
        before("G", [(sbuf, 0, width)], [])
        g.remote_dma(out_ap=T[dbuf][:, 0:width], in_ap=T[sbuf][:, 0:width], remote_sem=T.sem[dsem], local_sem=T.sem[lsem],
                     pid=pid, routing_id=rid, dma_engine_mask=topo.mask(core, dst))
        if lsem == "ls":
            ncall[0] += len(topo.engines(core, dst))

    NE = {d: len(topo.engines(T.cores[(rank + d) % n], core)) for d in (1, 2, -1, -2)}
    peer = {d: T.cores[(rank + d) % n] for d in (1, 2, -1, -2)}
    SLOT = {"a1": 1, "a2": 2, "b2": 1, "b0": -1, "c0": -2}
    for s, d in SLOT.items():
        landed(s + "v", s + "v_", NE[d])
        landed(s + "l", s + "l_", NE[d])
    landed("tab1", "t1", NE[1])
    landed("tab2", "t2", NE[2])

    cp(B("gx0"), X3("gli", EV, ALL))
    cp(B("gy0"), X3("gli", OD, ALL))
    cp(B("gx0", 128, 136), B("gx0", 0, 8))
    views(0)
    lists(0, B("gy0"))
    late_consts()
    cp(B("xsav", 0, 1), B("tab0", 2047, 2048))
    fill(B("tab0", 2047, 2048), FAR)
    send(peer[-1], "tab1", "t1", "tab0", 2048, "tl")
    send(peer[-2], "tab2", "t2", "tab0", 2048, "tl")
    tabtok = ("D", "tl", len(topo.engines(core, peer[-1])) + len(topo.engines(core, peer[-2])), {})
    after("D", [("tab0", 0, WT)], [], tabtok)
    iota(B("iw", 0, WT), [[1, WT]], 0, 0)

    def visit(t):
        s = t % 2
        gx, gy, abx, aby = "gx%d" % s, "gy%d" % s, "abx%d" % s, "aby%d" % s
        tab = "tab%d" % t
        for k in range(7):
            l, lo, hi = CH[k]
            w = (hi - lo) * 16
            d = "df%d" % k
            tt(B(d, 0, w), ind(B(tab, 0, 2048), B("off", l * 128 + lo, l * 128 + hi)), B("vx%d" % t, 0, w), A.subtract)
            if k == 3 and t == 0:
                cp(B("abx0", 0, 128), X3("ali", EV, ALL))
                cp(B("aby0", 0, 128), X3("ali", OD, ALL))
                cp(B("abx0", 128, 256), X3("bli", EV, ALL))
                cp(B("aby0", 128, 256), X3("bli", OD, ALL))
                cp(B("tha"), X3("thi", EV, ALL))
                cp(B("thb"), X3("thi", OD, ALL))
            act(B(d, 0, w), B(d, 0, w), F.Abs)
            if k == 3:
                act(B("sgx", 0, 128), B("b0"), F.Copy)
                act(B("sgx", 128, 136), B("b0", 0, 8), F.Copy)
                contract(3)
                if t == 0:
                    prepare(0)
            elif k == 5:
                act(B("sqy"), B("b1"), F.Copy)
                contract(5)
            elif k < 6:
                contract(k)
        tt(B("oyp", 8, 136), B("sqy"), B("b3", 128, 256), A.is_gt)
        tt(B("oxf"), B("sgx"), B("b3"), A.is_gt)
        psum("b4", 0, [("idbig", "ex", 0, 0), ("idbig", "ey", 0, 0), ("idbig", "oyp", 8, 0)])
        tt(B("mn"), B("b1"), B("sgx"), A.min)
        cp(B("oyp", 0, 8), B("oyp", 128, 136))
        if t == 1:
            scatter("tab0", "lw0", "val0")
            scatter("tab2", "a2l", "a2v")
        if t == 2:
            scatter("tab0", "b0l", "b0v")
            cp(B("tab0", 2047, 2048), B("xsav", 0, 1))
        contract(6)
        tt(B("mnm"), B("mn"), B("b4"), A.subtract)
        tt(B("b7"), B("b2"), B("mnm"), A.is_ge)
        tt(B("mm"), B("b2"), B("mnm"), A.is_lt)
        for k in range(3):
            tt(X3("k0", k, ALL), B("b7"), B("kn", 128 * k, 128 * k + 128), A.add)
        for a, b, w in (("k0", "k1", 64), ("k1", "k2", 32), ("k2", "k3", 16), ("k3", "k4", 8)):
            tt(X3(b, ALL, ALL), X3(a, ALL, slice(0, w)), X3(a, ALL, slice(w, 2 * w)), A.min)
        tt(X3("k5", ALL, ALL), X3("k4", ALL, ALL), X3("fb", ALL, ALL), A.min)
        ts(B("ki", 0, 24), X3("k5", ALL, ALL), 2.0 ** 18, A.mult)
        ts(B("gi", 0, 24), B("ki", 0, 24), 4095, A.bitwise_and)
        cp(B("goff", 0, 24), B("gi", 0, 24))
        cp(B("gf", 0, 8), B("gi", 0, 8))
        act(B("xv", 0, 256), ind(B(tab, 0, 2048), B("goff", 8, 24)), F.Copy, scale=0.5, bias=-0.125)
        cp(B("bf"), ind(B("iw", 0, WT), B("goff", 0, 8)))
        tt(B("bd"), B("bf"), B("maskd"), A.max)
        for c in range(1, 8):
            ts(B("eq", 128 * c, 128 * c + 16 * c), B("bf", 0, 16 * c), B("gf", c, c + 1), A.is_equal)
        val, lw = "val%d" % t, "lw%d" % t
        tt(B("vi"), B("xv", 0, 128), B("xv", 128, 256), A.add)
        for c in range(8):
            ts(B("eq", 144 * c, 144 * c + 16), B("bd", 16 * c, 16 * c + 16), B("gf", c, c + 1), A.is_equal)
        cp(B(val), B("vi"))
        e, z, r = B("eq", 0, 1024), B("sc", 0, 1024), B("rst", 0, 1024)
        do("V", [z], [e, r], lambda q: q.tensor_tensor_scan(out=z[0], data0=r[0], data1=e[0], initial=0.0, op0=A.mult, op1=A.max))
        tt(B("lm", 0, 8), ST("sc", 127, 1024, 128), B("dum", 0, 8), A.mult)
        tt(B("lf", 0, 8), B("lm", 0, 8), B("gf", 0, 8), A.max)
        cp(B(lw, 0, 8), B("lf", 0, 8))
        for slot, d in ((("a1", -1), ("a2", -2)), (("b2", -1), ("b0", 1)), (("c0", 2),))[t]:
            send(peer[d], slot + "v", slot + "v_", val, 128)
            send(peer[d], slot + "l", slot + "l_", lw, 8)
        psum("b4", 128, [("idbig", "ey", 0, 0), ("idbig", "ones", 0, 0), ("idnbig", "ex", 0, 0), ("idbig", "oyp", 0, 0)])
        psum("b4", 256, [("idbig", "ones", 0, 0), ("idnbig", "ey", 0, 0), ("idbig", "oxf", 0, 0), ("idbig", "ex", 8, 0)])
        tt(B("mt"), B("sqy"), B("b4", 128, 256), A.subtract)
        tt(B("b7", 128, 256), B("sgx", 8, 136), B("b4", 256, 384), A.subtract)
        tt(B("tx"), B("b2"), B("mt"), A.is_lt)
        tt(B("ty"), B("sqy"), B("b7", 128, 256), A.is_lt)
        tt(B("p1"), B("b5"), B("oxf"), A.mult)
        tt(B("p2"), B("b5", 128, 256), B("oyp", 0, 128), A.mult)
        tt(B("p3"), B("b5", 256, 384), B("mm"), A.mult)
        tt(B("p4_"), B("b6"), B("oyp", 8, 136), A.mult)
        tt(B("p5"), B("b5", 384, 512), B("oxf"), A.mult)
        tt(B("p6"), B("b6", 256, 384), B("mm"), A.mult)
        tt(B("p7"), B("b6", 128, 256), B("ty"), A.mult)
        tt(B("p8"), B("b5", 256, 384), B("tx"), A.mult)
        ry, rx = ((0, 1), (-1, 0), (0, 0))[t]
        ny = [("id1", b, 0, ry) for b in (gy, "p4_", "p5", "p6", "p7")]
        nx = [("id1", b, 0, rx) for b in (gx, "p1", "p2", "p3", "p8")]
        psum("b0", 0, ny)
        psum("b0", 128, nx)
        psum("b3", 0, [("id2047", "oxf", 0, 0), ("id2047", "oyp", 0, 0), ("id2047", "tx", 0, 0), ("id2047", "mm", 0, 0)])
        psum("b3", 128, [("id2047", "ones", 0, 0), ("idn2047", "mm", 0, 0)])
        psum("b3", 256, [("id2047", "oyp", 8, 0), ("id2047", "oxf", 0, 0), ("id2047", "ty", 0, 0), ("id2047", "mm", 0, 0)])
        if t < 2:
            u = 1 - s
            hx, hy = "gx%d" % u, "gy%d" % u
            cp(B(hx), B("b0"))
            cp(B(hy), B("b0", 128, 256))
            cp(B(hx, 128, 136), B(hx, 0, 8))
            lists(t + 1, B("b0", 128, 256))
            cp(B("mm", 128, 256), B("mm"))
            for k in range(16):
                mm(B("b2", 384, 512), B("rr"), B("mm", 8 * k, 8 * k + 128), k == 0, k == 15)
            act(B("cs"), B("b2", 384, 512), F.Copy)
            views(t + 1)
        else:
            act(X3("ogs", OD, ALL), B("b0"), F.Copy)
            act(X3("ogs", EV, ALL), B("b0", 128, 256), F.Copy)
            before("Y", [("ogs", 0, 9)], [])
            g.sync.dma_start(out=T.og[:, :], in_=T.ogs[:, :, :]).then_inc(T.sem.og_, 16)
        tt(B("b7", 256, 384), B("b3", 128, 256), B(gx), A.max)
        tt(B("b7", 384, 512), B("b3", 128, 256), B(gy), A.max)
        tt(B("ab2", 0, 128), B("b3"), B(abx), A.max)
        tt(B("ab2", 128, 256), B("b3"), B(abx, 128, 256), A.max)
        if t < 2:
            nax, nay = "abx%d" % u, "aby%d" % u
            for o in (0, 128):
                for a, b in ((0, 120), (120, 128)) if t == 0 else ((0, 128),):
                    d = (a - 8 * rx) % U
                    d, a2, b2 = (o + a, o + (a + 8) % U, 0) if t == 0 else (o, o, 0)
                    w = b - a
                    tt(B(nay, d, d + w), B("b7", 256 + a2, 256 + a2 + w), B("ab2", a2, a2 + w), A.min)
                for a, b in ((0, 8), (8, 128)) if t == 1 else ((0, 128),):
                    w = b - a
                    sr = (a - 8) % U if t == 1 else a
                    tt(B(nax, o + a, o + b), B("b3", 256 + sr, 256 + sr + w), B(aby, o + sr, o + sr + w), A.max)
            prepare(t + 1)
        else:
            for o, b, q, sm in ((0, "oas", T.oa, "oa_"), (128, "obs", T.ob, "ob_")):
                tt(X3(b, EV, ALL), B("b7", 256 + o, 384 + o), B("ab2", o, o + 128), A.min)
                tt(X3(b, OD, ALL), B("b3", 256, 384), B(aby, o, o + 128), A.max)
                before("Y", [(b, 0, 9)], [])
                g.sync.dma_start(out=q[:, :], in_=T[b][:, :, :]).then_inc(T.sem[sm], 16)

    visit(0)
    scatter("tab1", "a1l", "a1v")
    visit(1)
    scatter("tab2", "b2l", "b2v")
    visit(2)
    scatter("tab0", "c0l", "c0v")
    before("Y", [("tab0", 0, 2048)], [])
    g.sync.dma_start(out=T.ox[:, :], in_=T.tab0[:, 0:2048]).then_inc(T.sem.ox_, 16)
    for sm in ("og_", "oa_", "ob_", "ox_"):
        g.sync.wait_ge(T.sem[sm], 16)
    for e in ("V", "S", "P", "G"):
        g.wait_ge(T.sem[PS[e]], cnt[e])
    g.wait_ge(T.sem.ls, ncall[0])
